import numpy as np
import ml_dtypes


def mxq(x, axis, fmt="e4m3"):
    dtype, down = {"e4m3": (ml_dtypes.float8_e4m3fn, 7), "e5m2": (ml_dtypes.float8_e5m2, 14)}[fmt]
    v = np.moveaxis(np.asarray(x, np.float32).astype(ml_dtypes.bfloat16).astype(np.float64), axis, -1)
    blocks = v.reshape(v.shape[:-1] + (-1, 32))
    amax = np.abs(blocks).max(-1, keepdims=True)
    byte = np.maximum(np.where(amax > 0, np.frexp(amax)[1] - 1 + 127, 0) - down, 1)
    scale = np.exp2(byte - 127.0)
    codes = (blocks / scale).astype(np.float32).astype(dtype).astype(np.float64)
    return np.moveaxis((codes * scale).reshape(v.shape), -1, axis)


WIDE = False


def mx_kscale(k):
    if not WIDE:
        return np.ones(k)
    levels = np.array([10, -10, 5, -5, 0])
    if k % 512:
        return np.exp2(np.random.permutation(np.resize(levels, k // 32))).repeat(32)
    a = np.empty((k // 512, 16))
    for p in range(k // 512):
        a[p, :8] = np.random.permutation(np.resize(levels, 8))
        for g in range(8):
            far = levels[np.abs(levels - a[p, g]) >= 10]
            a[p, g + 8] = far[np.random.randint(len(far))]
    return np.exp2(a.ravel()).repeat(32)


def f64(x):
    return np.asarray(x).astype(np.float64)


def striped(idx):
    return np.tile(idx.reshape(-1, 16).T, (8, 1)).astype(np.uint16)


def unstriped(offs):
    return offs[:16].T.reshape(-1).astype(np.int64)


def pack_weight(w):
    k, n = w.shape
    w = f64(np.asarray(w, np.float32).astype(ml_dtypes.bfloat16)).reshape(k // 32, 32, n)
    amax = np.abs(w).max(1)
    byte = np.clip(np.where(amax > 0, np.frexp(amax)[1] - 1 + 127 - 7, 1), 1, 254)
    scaled = (w * np.exp2(127.0 - byte)[:, None, :]).reshape(k, n).astype(np.float32)
    words = np.ascontiguousarray(scaled.reshape(k // 512, 128, 4, n).transpose(0, 1, 3, 2)).astype(ml_dtypes.float8_e4m3fn).view(np.uint8)
    return words, np.ascontiguousarray(byte.astype(np.uint8).reshape(k // 512, 16, n))


def unpack_weight(words, scales):
    g, p, n, _ = words.shape
    vals = np.ascontiguousarray(words).view(ml_dtypes.float8_e4m3fn).astype(np.float64) * np.repeat(np.exp2(scales.astype(np.float64) - 127.0), 8, axis=1)[..., None]
    return vals.transpose(0, 1, 3, 2).reshape(g * 512, n)


K, T, S, N, H, W, U = 512, 2048, 512, 256, 512, 1024, 1024


def setup_inputs():
    n = np.random.standard_normal
    s = mx_kscale(K)[:, None]
    u = mx_kscale(H)
    packed_xT = pack_weight(n((K, T)) * s)
    packed_eT = pack_weight(n((K, W)) * s)
    return {
        "x_words": packed_xT[0],
        "x_scales": packed_xT[1],
        "w1": (n((K, H)) / np.sqrt(K) / s).astype(np.float32),
        "e_words": packed_eT[0],
        "e_scales": packed_eT[1],
        "w2": (n((K, H)) / np.sqrt(K) / s).astype(np.float32),
        "att": (np.random.uniform(0.3, 1.4, (H, U))).astype(np.float32),
        "unit": (np.random.uniform(0.6, 1.4, (H, 1)) * u[:, None]).astype(np.float32),
        "w3": (n((H, N)) / np.sqrt(H) / u[:, None]).astype(np.float32),
        "offs": striped(np.random.permutation(T)[:S]),
        "ski": striped(np.random.permutation(W)[:S]),
        "ex": striped(np.random.permutation(np.concatenate([np.arange(S), np.random.randint(0, S, U - S)]))),
        "sk1": striped(np.random.permutation(np.concatenate([np.arange(S), np.random.randint(0, S, U - S)]))),
        "sk2": striped(np.random.permutation(np.concatenate([np.arange(S), np.random.randint(0, S, U - S)]))),
    }


def reference(x_words, x_scales, w1, e_words, e_scales, w2, att, unit, w3, offs, ski, ex, sk1, sk2):
    xq = unpack_weight(x_words, x_scales)[:, unstriped(offs)]
    y = mxq(f64(w1), 0, "e4m3").T @ xq
    y_1 = y[:, unstriped(ex)]
    e_ski = unpack_weight(e_words, e_scales)[:, unstriped(ski)]
    ye = mxq(f64(w2), 0, "e4m3").T @ e_ski
    e_1 = ye[:, unstriped(sk1)]
    mas = y_1 + e_1
    e_2 = ye[:, unstriped(sk2)]
    hid = f64(unit) * (mas * f64(att) - (e_2 * e_1))
    return mxq(f64(w3), 0, "e4m3").T @ mxq(hid, 0, "e4m3")

@@ -1,0 +1,187 @@
+from contextlib import ExitStack
+
+import concourse.mybir as mybir
+
+K, T, S, N, H, W, U = 512, 2048, 512, 256, 512, 1024, 1024
+FLOPS = 2 * K * H * S * 2 + 2 * H * N * U
+
+F32 = mybir.dt.float32
+BF16 = mybir.dt.bfloat16
+I32 = mybir.dt.int32
+U32 = mybir.dt.uint32
+U16 = mybir.dt.uint16
+U8 = mybir.dt.uint8
+FP8X4 = mybir.dt.float8_e4m3fn_x4
+ALU = mybir.AluOpType
+COPY = mybir.ActivationFunctionType.Copy
+
+P = 128
+PACK = 4
+PAD = 32
+HALF = 512
+CHUNKS = [(0, 512), (512, 256), (768, 256)]
+ON_VECTOR = [(0, 0), (0, 1)]
+
+
+def tile_picked_ytutorq_two_p_kernel(
+    tc, x_words, x_scales, w1, e_words, e_scales, w2, att, unit, w3, offs, ski, ex, sk1, sk2, out
+):
+    nc = tc.nc
+    with ExitStack() as ctx:
+        keep = ctx.enter_context(tc.tile_pool(name="keep", bufs=1))
+        psum = ctx.enter_context(tc.psum_pool(name="psum", bufs=1))
+
+        def load_list(src, name):
+            t = keep.tile([P, src.shape[1]], U16, name=name)
+            nc.sync.dma_start(t[:], src)
+            return t
+
+        def load_scales(src, cols, name):
+            t = keep.tile([P, cols], U8, name=name, align_bytes=64)
+            for q in range(4):
+                rows = src[0, 4 * q : 4 * q + 4, :].bitcast(I32)
+                nc.sync.dma_start(t[32 * q : 32 * q + 32, :].bitcast(I32), rows.partition_broadcast(8))
+            return t
+
+        def load_words(src, cols, name):
+            t = keep.tile([P, cols], I32, name=name, align_bytes=64)
+            nc.sync.dma_start(t[:], src[0].rearrange("p n t -> p (n t)").bitcast(I32))
+            return t
+
+        def load_w(src, name):
+            t = keep.tile([P, PACK, H], F32, name=name)
+            nc.sync.dma_start(t[:], src.rearrange("(p j) c -> p j c", j=PACK))
+            return t
+
+        att_v = att.rearrange("(g t j) r -> t g j r", t=PACK, j=8)
+        w3_v = w3.rearrange("(g t j) m -> t g j m", t=PACK, j=8)
+        unit_v = unit.rearrange("(g t j) o -> t g j o", t=PACK, j=8)
+
+        def load_att(t):
+            a = keep.tile([P, U], F32, name=f"att{t}")
+            nc.sync.dma_start(a[:], att_v[t])
+            return a
+
+        ski_sb = load_list(ski, "ski_sb")
+        e_sc = load_scales(e_scales, W, "e_sc")
+        e_wd = load_words(e_words, W, "e_wd")
+        w2_raw = load_w(w2, "w2_raw")
+        sk2_sb = load_list(sk2, "sk2_sb")
+        sk1_sb = load_list(sk1, "sk1_sb")
+        att_sb = [load_att(0), load_att(1)]
+        unit_sb = [keep.tile([P, 1], F32, name=f"unit{t}") for t in range(PACK)]
+        for t in range(PACK):
+            nc.sync.dma_start(unit_sb[t][:], unit_v[t])
+        offs_sb = load_list(offs, "offs_sb")
+        x_sc = load_scales(x_scales, T, "x_sc")
+        x_wd = load_words(x_words, T, "x_wd")
+        w1_raw = load_w(w1, "w1_raw")
+        att_sb.extend([load_att(2), load_att(3)])
+        ex_sb = load_list(ex, "ex_sb")
+        w3_raw = keep.tile([P, PACK, N], F32, name="w3_raw")
+        for t in range(PACK):
+            nc.sync.dma_start(w3_raw[:, t, :], w3_v[t])
+
+        neg_ye = [keep.tile([P, S + PAD], F32, name=f"neg_ye{t}") for t in range(PACK)]
+        y_unit = [keep.tile([P, S + PAD], F32, name=f"y_unit{t}") for t in range(PACK)]
+        for win in neg_ye + y_unit:
+            nc.gpsimd.memset(win[:, S:], 0.0)
+
+        def quant_w(raw, name, t, copy):
+            grouped = keep.tile([P, P * PACK], BF16, name=f"{name}_bf{t}", align_bytes=64)
+            copy(
+                grouped[:].rearrange("p (g c i k) -> p g c k i", g=16, c=2, i=4),
+                raw[:].rearrange("p k (g t c i) -> p t g c k i", t=PACK, c=2, i=4)[:, t],
+            )
+            codes = keep.tile([P, P], U32, name=f"{name}_codes{t}", align_bytes=64)
+            scales = keep.tile([P, P], U8, name=f"{name}_scales{t}", align_bytes=64)
+            nc.vector.quantize_mx(out=codes[:].bitcast(FP8X4), scales=scales[:], in_=grouped[:])
+            return codes, scales
+
+        def pick(words, scales, lst, name):
+            pw = keep.tile([P, S], U32, name=f"{name}_pw", align_bytes=64)
+            ps = keep.tile([P, S], U8, name=f"{name}_ps", align_bytes=64)
+            nc.vector.tensor_copy(ps[:], scales[:].indirect(lst[:]))
+            nc.vector.tensor_copy(pw[:], words[:].bitcast(U32).indirect(lst[:]))
+            return pw, ps
+
+        def product(wq, picked, bank, width):
+            acc = psum.tile([P, width], F32, name=f"bank{bank}")
+            nc.tensor.matmul_mx(
+                out=acc[:], lhsT=wq[0][:].bitcast(FP8X4), lhsT_scale=wq[1][:],
+                rhs=picked[0][:].bitcast(FP8X4), rhs_scale=picked[1][:], start=True, stop=True,
+            )
+            return acc
+
+        e_pick = pick(e_wd, e_sc, ski_sb, "e")
+        ye_acc = []
+        for t in range(PACK):
+            w2q = quant_w(w2_raw, "w2", t, nc.vector.tensor_copy if t % 2 == 0 else nc.scalar.copy)
+            ye_acc.append(product(w2q, e_pick, t, S))
+
+        cols = HALF // 16
+        skill = keep.tile([P, PACK, U], F32, name="skill")
+
+        def skill_part(t):
+            nc.scalar.activation(neg_ye[t][:, :S], ye_acc[t][:], COPY, scale=-1.0)
+            parts = []
+            for h in range(2):
+                r = slice(h * HALF, (h + 1) * HALF)
+                c = slice(h * cols, (h + 1) * cols)
+                neg_e1 = keep.tile([P, HALF], F32, name=f"neg_e1_{h}{t}")
+                nc.scalar.activation(neg_e1[:], neg_ye[t][:].indirect(sk1_sb[:, c]), COPY)
+                rest = keep.tile([P, HALF], F32, name=f"rest_{h}{t}")
+                nc.vector.tensor_tensor(rest[:], neg_ye[t][:].indirect(sk2_sb[:, c]), att_sb[t][:, r], ALU.add)
+                parts.append((r, neg_e1, rest))
+            for r, neg_e1, rest in parts:
+                nc.vector.scalar_tensor_tensor(skill[:, t, r], neg_e1[:], unit_sb[t][:], rest[:], ALU.mult, ALU.mult)
+
+        skill_part(0)
+        x_pick = pick(x_wd, x_sc, offs_sb, "x")
+        skill_part(1)
+        y_acc = [product(quant_w(w1_raw, "w1", t, nc.scalar.copy), x_pick, PACK + t, S) for t in range(PACK)]
+        skill_part(2)
+        skill_part(3)
+        for t in range(PACK):
+            nc.scalar.activation(y_unit[t][:, :S], y_acc[t][:], COPY, scale=unit_sb[t][:])
+
+        w3_bf = keep.tile([P, N * PACK], BF16, name="w3_bf", align_bytes=64)
+        nc.scalar.copy(
+            w3_bf[:].rearrange("p (c i t) -> p c t i", i=4, t=PACK),
+            w3_raw[:].rearrange("p t (c i) -> p c t i", i=4),
+        )
+        w3_codes = keep.tile([P, N], U32, name="w3_codes", align_bytes=64)
+        w3_scales = keep.tile([P, N], U8, name="w3_scales", align_bytes=64)
+        nc.vector.quantize_mx(out=w3_codes[:].bitcast(FP8X4), scales=w3_scales[:], in_=w3_bf[:])
+
+        for h, (r0, width) in enumerate(CHUNKS):
+            r = slice(r0, r0 + width)
+            c = slice(r0 // 16, (r0 + width) // 16)
+            exer = keep.tile([P, PACK, width], F32, name=f"exer{h}")
+            for t in range(PACK):
+                window = y_unit[t][:].indirect(ex_sb[:, c])
+                if (h, t) in ON_VECTOR:
+                    nc.vector.tensor_tensor(exer[:, t, :], window, att_sb[t][:, r], ALU.mult)
+                else:
+                    y1 = keep.tile([P, width], F32, name=f"y1_{h}{t}")
+                    nc.scalar.activation(y1[:], window, COPY)
+                    nc.vector.tensor_tensor(exer[:, t, :], y1[:], att_sb[t][:, r], ALU.mult)
+            hid = keep.tile([P, width * PACK], BF16, name=f"hid{h}", align_bytes=64)
+            nc.vector.tensor_tensor(
+                hid[:].rearrange("p (c i t) -> p c t i", i=4, t=PACK),
+                exer[:].rearrange("p t (c i) -> p c t i", i=4),
+                skill[:, :, r].rearrange("p t (c i) -> p c t i", i=4),
+                ALU.subtract,
+            )
+            codes = keep.tile([P, width], U32, name=f"hid_codes{h}", align_bytes=64)
+            scales = keep.tile([P, width], U8, name=f"hid_scales{h}", align_bytes=64)
+            nc.vector.quantize_mx(out=codes[:].bitcast(FP8X4), scales=scales[:], in_=hid[:])
+            for m in range(N // P):
+                mc = slice(m * P, (m + 1) * P)
+                acc = product((w3_codes[:, mc], w3_scales[:, mc]), (codes, scales), 2 * h + m, width)
+                res = keep.tile([P, width], F32, name=f"res{h}{m}")
+                if h == len(CHUNKS) - 1 and m == 1:
+                    nc.vector.tensor_copy(res[:], acc[:])
+                else:
+                    nc.scalar.copy(res[:], acc[:])
+                nc.sync.dma_start(out[mc, r], res[:])

@@ -17,10 +17,14 @@ COPY = mybir.ActivationFunctionType.Copy
 
 P = 128
 PACK = 4
+GROUP = 8
+LIST_ROWS = 16
+MX_ALIGN = 64
+PAIR = 2
+HALF = U // 2
 PAD = 32
-HALF = 512
-CHUNKS = [(0, 512), (512, 256), (768, 256)]
-ON_VECTOR = [(0, 0), (0, 1)]
+EARLY = 2
+CHUNKS = [(0, 512), (512, 256), (768, 128), (896, 128)]
 
 
 def tile_picked_ytutorq_two_p_kernel(
@@ -32,156 +36,230 @@ def tile_picked_ytutorq_two_p_kernel(
         psum = ctx.enter_context(tc.psum_pool(name="psum", bufs=1))
 
         def load_list(src, name):
-            t = keep.tile([P, src.shape[1]], U16, name=name)
-            nc.sync.dma_start(t[:], src)
-            return t
+            entries = keep.tile([P, src.shape[1]], U16, name=name)
+            nc.sync.dma_start(entries[:], src)
+            return entries
 
         def load_scales(src, cols, name):
-            t = keep.tile([P, cols], U8, name=name, align_bytes=64)
+            plane = keep.tile([P, cols], U8, name=name, align_bytes=MX_ALIGN)
+            nc.gpsimd.memset(plane[:].bitcast(I32), 0)
             for q in range(4):
-                rows = src[0, 4 * q : 4 * q + 4, :].bitcast(I32)
-                nc.sync.dma_start(t[32 * q : 32 * q + 32, :].bitcast(I32), rows.partition_broadcast(8))
-            return t
+                nc.sync.dma_start(
+                    plane[32 * q : 32 * q + 4, :].bitcast(I32), src[0, 4 * q : 4 * q + 4, :].bitcast(I32)
+                )
+            return plane
 
         def load_words(src, cols, name):
-            t = keep.tile([P, cols], I32, name=name, align_bytes=64)
-            nc.sync.dma_start(t[:], src[0].rearrange("p n t -> p (n t)").bitcast(I32))
-            return t
+            words = keep.tile([P, cols], I32, name=name, align_bytes=MX_ALIGN)
+            nc.sync.dma_start(words[:], src[0].rearrange("p n slot -> p (n slot)").bitcast(I32))
+            return words
 
-        def load_w(src, name):
-            t = keep.tile([P, PACK, H], F32, name=name)
-            nc.sync.dma_start(t[:], src.rearrange("(p j) c -> p j c", j=PACK))
-            return t
+        def load_weight(src, name):
+            raw = keep.tile([P, PACK, H], F32, name=name)
+            nc.sync.dma_start(raw[:], src.rearrange("(p slot) i -> p slot i", slot=PACK))
+            return raw
 
-        att_v = att.rearrange("(g t j) r -> t g j r", t=PACK, j=8)
-        w3_v = w3.rearrange("(g t j) m -> t g j m", t=PACK, j=8)
-        unit_v = unit.rearrange("(g t j) o -> t g j o", t=PACK, j=8)
+        def row_tile(src, t):
+            return src.rearrange("(g t j) c -> t g j c", t=PACK, j=GROUP)[t]
 
-        def load_att(t):
-            a = keep.tile([P, U], F32, name=f"att{t}")
-            nc.sync.dma_start(a[:], att_v[t])
-            return a
+        def load_rows(src, t, name):
+            rows = keep.tile([P, src.shape[1]], F32, name=f"{name}{t}")
+            nc.sync.dma_start(rows[:], row_tile(src, t))
+            return rows
 
         ski_sb = load_list(ski, "ski_sb")
-        e_sc = load_scales(e_scales, W, "e_sc")
-        e_wd = load_words(e_words, W, "e_wd")
-        w2_raw = load_w(w2, "w2_raw")
+        e_words_sb = load_words(e_words, W, "e_words_sb")
+        e_scales_sb = load_scales(e_scales, W, "e_scales_sb")
+        w2_raw = load_weight(w2, "w2_raw")
+        att_sb = [load_rows(att, 0, "att")]
         sk2_sb = load_list(sk2, "sk2_sb")
         sk1_sb = load_list(sk1, "sk1_sb")
-        att_sb = [load_att(0), load_att(1)]
-        unit_sb = [keep.tile([P, 1], F32, name=f"unit{t}") for t in range(PACK)]
-        for t in range(PACK):
-            nc.sync.dma_start(unit_sb[t][:], unit_v[t])
+        unit_sb = [load_rows(unit, 0, "unit")]
+        att_sb.append(load_rows(att, 1, "att"))
+        unit_sb.append(load_rows(unit, 1, "unit"))
+        w1_raw = load_weight(w1, "w1_raw")
         offs_sb = load_list(offs, "offs_sb")
-        x_sc = load_scales(x_scales, T, "x_sc")
-        x_wd = load_words(x_words, T, "x_wd")
-        w1_raw = load_w(w1, "w1_raw")
-        att_sb.extend([load_att(2), load_att(3)])
+        x_scales_sb = load_scales(x_scales, T, "x_scales_sb")
+        x_words_sb = load_words(x_words, T, "x_words_sb")
+        for t in range(EARLY, PACK):
+            att_sb.append(load_rows(att, t, "att"))
+            unit_sb.append(load_rows(unit, t, "unit"))
         ex_sb = load_list(ex, "ex_sb")
         w3_raw = keep.tile([P, PACK, N], F32, name="w3_raw")
         for t in range(PACK):
-            nc.sync.dma_start(w3_raw[:, t, :], w3_v[t])
+            nc.sync.dma_start(w3_raw[:, t, :], row_tile(w3, t))
 
         neg_ye = [keep.tile([P, S + PAD], F32, name=f"neg_ye{t}") for t in range(PACK)]
         y_unit = [keep.tile([P, S + PAD], F32, name=f"y_unit{t}") for t in range(PACK)]
-        for win in neg_ye + y_unit:
-            nc.gpsimd.memset(win[:, S:], 0.0)
+        for window in neg_ye + y_unit:
+            nc.gpsimd.memset(window[:, S:], 0.0)
 
-        def quant_w(raw, name, t, copy):
-            grouped = keep.tile([P, P * PACK], BF16, name=f"{name}_bf{t}", align_bytes=64)
+        def round_weight(raw, t, grouped, copy):
             copy(
-                grouped[:].rearrange("p (g c i k) -> p g c k i", g=16, c=2, i=4),
-                raw[:].rearrange("p k (g t c i) -> p t g c k i", t=PACK, c=2, i=4)[:, t],
+                grouped.rearrange("p (g c n slot) -> p g c slot n", slot=PACK, n=PAIR, c=GROUP // PAIR),
+                raw[:].rearrange("p slot (g t c n) -> p t g c slot n", t=PACK, n=PAIR, c=GROUP // PAIR)[:, t],
             )
-            codes = keep.tile([P, P], U32, name=f"{name}_codes{t}", align_bytes=64)
-            scales = keep.tile([P, P], U8, name=f"{name}_scales{t}", align_bytes=64)
-            nc.vector.quantize_mx(out=codes[:].bitcast(FP8X4), scales=scales[:], in_=grouped[:])
+
+        def quantise(grouped, name, codes_buffer):
+            width = grouped.shape[1] // PACK
+            codes = keep.tile([P, width], U32, name=codes_buffer, align_bytes=MX_ALIGN)
+            scales = keep.tile([P, width], U8, name=f"{name}_scales", align_bytes=MX_ALIGN)
+            nc.vector.quantize_mx(out=codes[:].bitcast(FP8X4), scales=scales[:], in_=grouped)
             return codes, scales
 
-        def pick(words, scales, lst, name):
-            pw = keep.tile([P, S], U32, name=f"{name}_pw", align_bytes=64)
-            ps = keep.tile([P, S], U8, name=f"{name}_ps", align_bytes=64)
-            nc.vector.tensor_copy(ps[:], scales[:].indirect(lst[:]))
-            nc.vector.tensor_copy(pw[:], words[:].bitcast(U32).indirect(lst[:]))
-            return pw, ps
+        def pick_words(words, entries, name):
+            picked = keep.tile([P, S], U32, name=name, align_bytes=MX_ALIGN)
+            nc.vector.tensor_copy(picked[:], words[:].bitcast(U32).indirect(entries[:]))
+            return picked
 
-        def product(wq, picked, bank, width):
+        def pick_scales(plane, entries, name):
+            picked = keep.tile([P, S], U8, name=name, align_bytes=MX_ALIGN)
+            nc.vector.tensor_copy(picked[:], plane[:].indirect(entries[:]))
+            return picked
+
+        def product(stationary, moving, bank, width):
             acc = psum.tile([P, width], F32, name=f"bank{bank}")
             nc.tensor.matmul_mx(
-                out=acc[:], lhsT=wq[0][:].bitcast(FP8X4), lhsT_scale=wq[1][:],
-                rhs=picked[0][:].bitcast(FP8X4), rhs_scale=picked[1][:], start=True, stop=True,
+                out=acc[:],
+                lhsT=stationary[0][:].bitcast(FP8X4),
+                lhsT_scale=stationary[1][:],
+                rhs=moving[0][:].bitcast(FP8X4),
+                rhs_scale=moving[1][:],
+                start=True,
+                stop=True,
             )
             return acc
 
-        e_pick = pick(e_wd, e_sc, ski_sb, "e")
-        ye_acc = []
+        def entries_of(list_sb, first, count):
+            return list_sb[:, first // LIST_ROWS : (first + count) // LIST_ROWS]
+
+        def interleaved(rows_by_tile):
+            return rows_by_tile.rearrange("p t (c n) -> p c t n", n=PAIR)
+
+        def as_words(grouped):
+            return grouped.rearrange("p (c n t) -> p c t n", n=PAIR, t=PACK)
+
+        e_picked = (pick_words(e_words_sb, ski_sb, "e_picked_words"), pick_scales(e_scales_sb, ski_sb, "e_picked_scales"))
+        ye_acc = {}
+        w2_bf = []
         for t in range(PACK):
-            w2q = quant_w(w2_raw, "w2", t, nc.vector.tensor_copy if t % 2 == 0 else nc.scalar.copy)
-            ye_acc.append(product(w2q, e_pick, t, S))
+            w2_bf.append(keep.tile([P, P * PACK], BF16, name=f"w2_bf{t}", align_bytes=MX_ALIGN))
+            round_weight(w2_raw, t, w2_bf[t][:], nc.vector.tensor_copy if t % 2 == 0 else nc.scalar.copy)
 
-        cols = HALF // 16
-        skill = keep.tile([P, PACK, U], F32, name="skill")
+        def skill_product(t, codes_buffer):
+            ye_acc[t] = product(quantise(w2_bf[t][:], f"w2_{t}", codes_buffer), e_picked, t, S)
 
-        def skill_part(t):
-            nc.scalar.activation(neg_ye[t][:, :S], ye_acc[t][:], COPY, scale=-1.0)
-            parts = []
-            for h in range(2):
-                r = slice(h * HALF, (h + 1) * HALF)
-                c = slice(h * cols, (h + 1) * cols)
-                neg_e1 = keep.tile([P, HALF], F32, name=f"neg_e1_{h}{t}")
-                nc.scalar.activation(neg_e1[:], neg_ye[t][:].indirect(sk1_sb[:, c]), COPY)
-                rest = keep.tile([P, HALF], F32, name=f"rest_{h}{t}")
-                nc.vector.tensor_tensor(rest[:], neg_ye[t][:].indirect(sk2_sb[:, c]), att_sb[t][:, r], ALU.add)
-                parts.append((r, neg_e1, rest))
-            for r, neg_e1, rest in parts:
-                nc.vector.scalar_tensor_tensor(skill[:, t, r], neg_e1[:], unit_sb[t][:], rest[:], ALU.mult, ALU.mult)
+        for t in range(EARLY):
+            skill_product(t, f"w2_codes{t}")
 
-        skill_part(0)
-        x_pick = pick(x_wd, x_sc, offs_sb, "x")
-        skill_part(1)
-        y_acc = [product(quant_w(w1_raw, "w1", t, nc.scalar.copy), x_pick, PACK + t, S) for t in range(PACK)]
-        skill_part(2)
-        skill_part(3)
+        skill = [keep.tile([P, PACK, HALF], F32, name=f"skill{half}") for half in range(2)]
+        rest = {}
+
+        def skill_rest(t, half):
+            if half == 0:
+                nc.scalar.activation(neg_ye[t][:, :S], ye_acc[t][:], COPY, scale=-1.0)
+            rest[t, half] = keep.tile([P, HALF], F32, name=f"rest{t}_{half}", align_bytes=MX_ALIGN)
+            neg_e2 = neg_ye[t][:].indirect(entries_of(sk2_sb, half * HALF, HALF))
+            nc.vector.tensor_tensor(rest[t, half][:], neg_e2, att_sb[t][:, half * HALF : (half + 1) * HALF], ALU.add)
+
+        def skill_term(t, half, buffer):
+            neg_e1 = keep.tile([P, HALF], F32, name=buffer, align_bytes=MX_ALIGN)
+            nc.scalar.activation(neg_e1[:], neg_ye[t][:].indirect(entries_of(sk1_sb, half * HALF, HALF)), COPY)
+            nc.vector.scalar_tensor_tensor(
+                skill[half][:, t, :], neg_e1[:], unit_sb[t][:], rest[t, half][:], ALU.mult, ALU.mult
+            )
+
+        def skill_tile(t):
+            for half in range(2):
+                skill_rest(t, half)
+            for half in range(2):
+                skill_term(t, half, f"neg_e1_{t}_{half}")
+
+        for t in range(EARLY):
+            skill_tile(t)
+
+        last = EARLY - 1
+        for t in range(EARLY, PACK):
+            skill_product(t, f"neg_e1_{last}_{t - EARLY}")
+
+        x_scales_picked = pick_scales(x_scales_sb, offs_sb, "x_picked_scales")
+        x_picked = (pick_words(x_words_sb, offs_sb, "x_picked_words"), x_scales_picked)
+        w1_bf = keep.tile([P, H * PACK], BF16, name="w1_bf", align_bytes=MX_ALIGN)
+        for t in range(PACK):
+            round_weight(w1_raw, t, w1_bf[:, t * P * PACK : (t + 1) * P * PACK], nc.scalar.copy)
+        w1_codes, w1_scales = quantise(w1_bf[:], "w1", f"rest{last}_0")
+        y_acc = []
+        for t in range(PACK):
+            tile_cols = slice(t * P, (t + 1) * P)
+            y_acc.append(product((w1_codes[:, tile_cols], w1_scales[:, tile_cols]), x_picked, PACK + t, S))
+
+        for t in range(EARLY, PACK):
+            skill_rest(t, 0)
+        for t in range(EARLY, PACK):
+            skill_term(t, 0, f"neg_e1_{t}_0")
         for t in range(PACK):
             nc.scalar.activation(y_unit[t][:, :S], y_acc[t][:], COPY, scale=unit_sb[t][:])
+        for t in range(EARLY, PACK):
+            skill_rest(t, 1)
 
-        w3_bf = keep.tile([P, N * PACK], BF16, name="w3_bf", align_bytes=64)
-        nc.scalar.copy(
-            w3_bf[:].rearrange("p (c i t) -> p c t i", i=4, t=PACK),
-            w3_raw[:].rearrange("p t (c i) -> p c t i", i=4),
-        )
-        w3_codes = keep.tile([P, N], U32, name="w3_codes", align_bytes=64)
-        w3_scales = keep.tile([P, N], U8, name="w3_scales", align_bytes=64)
-        nc.vector.quantize_mx(out=w3_codes[:].bitcast(FP8X4), scales=w3_scales[:], in_=w3_bf[:])
+        w3_codes = keep.tile([P, N], U32, name="w3_codes", align_bytes=MX_ALIGN)
+        w3_scales = keep.tile([P, N], U8, name="w3_scales", align_bytes=MX_ALIGN)
+        exercise = [keep.tile([P, PACK, count], F32, name=f"exercise{c}") for c, (first, count) in enumerate(CHUNKS)]
+        hid = [
+            keep.tile([P, count * PACK], BF16, name=f"hid{c}", align_bytes=MX_ALIGN)
+            for c, (first, count) in enumerate(CHUNKS)
+        ]
 
-        for h, (r0, width) in enumerate(CHUNKS):
-            r = slice(r0, r0 + width)
-            c = slice(r0 // 16, (r0 + width) // 16)
-            exer = keep.tile([P, PACK, width], F32, name=f"exer{h}")
-            for t in range(PACK):
-                window = y_unit[t][:].indirect(ex_sb[:, c])
-                if (h, t) in ON_VECTOR:
-                    nc.vector.tensor_tensor(exer[:, t, :], window, att_sb[t][:, r], ALU.mult)
-                else:
-                    y1 = keep.tile([P, width], F32, name=f"y1_{h}{t}")
-                    nc.scalar.activation(y1[:], window, COPY)
-                    nc.vector.tensor_tensor(exer[:, t, :], y1[:], att_sb[t][:, r], ALU.mult)
-            hid = keep.tile([P, width * PACK], BF16, name=f"hid{h}", align_bytes=64)
+        def exercise_term(c, t):
+            first, count = CHUNKS[c]
+            y_1 = y_unit[t][:].indirect(entries_of(ex_sb, first, count))
+            if (c, t) != (0, 0):
+                gathered = keep.tile([P, count], F32, name=f"y_1_{c}_{t}", align_bytes=MX_ALIGN)
+                nc.scalar.activation(gathered[:], y_1, COPY)
+                y_1 = gathered[:]
+            nc.vector.tensor_tensor(exercise[c][:, t, :], y_1, att_sb[t][:, first : first + count], ALU.mult)
+
+        def quantise_w3(buffer):
+            w3_bf = keep.tile([P, N * PACK], BF16, name=buffer, align_bytes=MX_ALIGN)
+            nc.scalar.copy(as_words(w3_bf[:]), interleaved(w3_raw[:]))
+            nc.vector.quantize_mx(out=w3_codes[:].bitcast(FP8X4), scales=w3_scales[:], in_=w3_bf[:])
+
+        def combine(c):
+            first, count = CHUNKS[c]
+            skill_cols = skill[first // HALF][:, :, first % HALF : first % HALF + count]
             nc.vector.tensor_tensor(
-                hid[:].rearrange("p (c i t) -> p c t i", i=4, t=PACK),
-                exer[:].rearrange("p t (c i) -> p c t i", i=4),
-                skill[:, :, r].rearrange("p t (c i) -> p c t i", i=4),
-                ALU.subtract,
+                as_words(hid[c][:]), interleaved(exercise[c][:]), interleaved(skill_cols), ALU.subtract
             )
-            codes = keep.tile([P, width], U32, name=f"hid_codes{h}", align_bytes=64)
-            scales = keep.tile([P, width], U8, name=f"hid_scales{h}", align_bytes=64)
-            nc.vector.quantize_mx(out=codes[:].bitcast(FP8X4), scales=scales[:], in_=hid[:])
+
+        def finish(c):
+            first, count = CHUNKS[c]
+            hid_mx = quantise(hid[c][:], f"hid{c}", f"hid{c}_codes")
             for m in range(N // P):
-                mc = slice(m * P, (m + 1) * P)
-                acc = product((w3_codes[:, mc], w3_scales[:, mc]), (codes, scales), 2 * h + m, width)
-                res = keep.tile([P, width], F32, name=f"res{h}{m}")
-                if h == len(CHUNKS) - 1 and m == 1:
-                    nc.vector.tensor_copy(res[:], acc[:])
+                rows = slice(m * P, (m + 1) * P)
+                acc = product((w3_codes[:, rows], w3_scales[:, rows]), hid_mx, (N // P) * c + m, count)
+                result = keep.tile([P, count], F32, name=f"result{c}_{m}")
+                if c == len(CHUNKS) - 1 and m == N // P - 1:
+                    nc.vector.tensor_copy(result[:], acc[:])
                 else:
-                    nc.scalar.copy(res[:], acc[:])
-                nc.sync.dma_start(out[mc, r], res[:])
+                    nc.scalar.copy(result[:], acc[:])
+                nc.sync.dma_start(out[rows, first : first + count], result[:])
+
+        for t in range(PACK):
+            exercise_term(0, t)
+        skill_term(EARLY, 1, "y_1_0_1")
+        combine(0)
+        skill_term(EARLY + 1, 1, "y_1_0_2")
+        quantise_w3("y_1_0_3")
+        finish(0)
+        exercise_term(1, 0)
+        exercise_term(1, 1)
+        for c in range(1, len(CHUNKS)):
+            more = c + 1 < len(CHUNKS)
+            exercise_term(c, 2)
+            exercise_term(c, 3)
+            if more:
+                exercise_term(c + 1, 0)
+            combine(c)
+            if more:
+                exercise_term(c + 1, 1)
+            finish(c)

from contextlib import ExitStack

import concourse.mybir as mybir

K, T, S, N, H, W, U = 512, 2048, 512, 256, 512, 1024, 1024
FLOPS = 2 * K * H * S * 2 + 2 * H * N * U

F32 = mybir.dt.float32
BF16 = mybir.dt.bfloat16
I32 = mybir.dt.int32
U32 = mybir.dt.uint32
U16 = mybir.dt.uint16
U8 = mybir.dt.uint8
FP8X4 = mybir.dt.float8_e4m3fn_x4
ALU = mybir.AluOpType
COPY = mybir.ActivationFunctionType.Copy

P = 128
PACK = 4
GROUP = 8
LIST_ROWS = 16
MX_ALIGN = 64
PAIR = 2
HALF = U // 2
PAD = 32
EARLY = 2
CHUNKS = [(0, 512), (512, 256), (768, 128), (896, 128)]


def tile_picked_ytutorq_two_p_kernel(
    tc, x_words, x_scales, w1, e_words, e_scales, w2, att, unit, w3, offs, ski, ex, sk1, sk2, out
):
    nc = tc.nc
    with ExitStack() as ctx:
        keep = ctx.enter_context(tc.tile_pool(name="keep", bufs=1))
        psum = ctx.enter_context(tc.psum_pool(name="psum", bufs=1))

        def load_list(src, name):
            entries = keep.tile([P, src.shape[1]], U16, name=name)
            nc.sync.dma_start(entries[:], src)
            return entries

        def load_scales(src, cols, name):
            plane = keep.tile([P, cols], U8, name=name, align_bytes=MX_ALIGN)
            nc.gpsimd.memset(plane[:].bitcast(I32), 0)
            for q in range(4):
                nc.sync.dma_start(
                    plane[32 * q : 32 * q + 4, :].bitcast(I32), src[0, 4 * q : 4 * q + 4, :].bitcast(I32)
                )
            return plane

        def load_words(src, cols, name):
            words = keep.tile([P, cols], I32, name=name, align_bytes=MX_ALIGN)
            nc.sync.dma_start(words[:], src[0].rearrange("p n slot -> p (n slot)").bitcast(I32))
            return words

        def load_weight(src, name):
            raw = keep.tile([P, PACK, H], F32, name=name)
            nc.sync.dma_start(raw[:], src.rearrange("(p slot) i -> p slot i", slot=PACK))
            return raw

        def row_tile(src, t):
            return src.rearrange("(g t j) c -> t g j c", t=PACK, j=GROUP)[t]

        def load_rows(src, t, name):
            rows = keep.tile([P, src.shape[1]], F32, name=f"{name}{t}")
            nc.sync.dma_start(rows[:], row_tile(src, t))
            return rows

        ski_sb = load_list(ski, "ski_sb")
        e_words_sb = load_words(e_words, W, "e_words_sb")
        e_scales_sb = load_scales(e_scales, W, "e_scales_sb")
        w2_raw = load_weight(w2, "w2_raw")
        att_sb = [load_rows(att, 0, "att")]
        sk2_sb = load_list(sk2, "sk2_sb")
        sk1_sb = load_list(sk1, "sk1_sb")
        unit_sb = [load_rows(unit, 0, "unit")]
        att_sb.append(load_rows(att, 1, "att"))
        unit_sb.append(load_rows(unit, 1, "unit"))
        w1_raw = load_weight(w1, "w1_raw")
        offs_sb = load_list(offs, "offs_sb")
        x_scales_sb = load_scales(x_scales, T, "x_scales_sb")
        x_words_sb = load_words(x_words, T, "x_words_sb")
        for t in range(EARLY, PACK):
            att_sb.append(load_rows(att, t, "att"))
            unit_sb.append(load_rows(unit, t, "unit"))
        ex_sb = load_list(ex, "ex_sb")
        w3_raw = keep.tile([P, PACK, N], F32, name="w3_raw")
        for t in range(PACK):
            nc.sync.dma_start(w3_raw[:, t, :], row_tile(w3, t))

        neg_ye = [keep.tile([P, S + PAD], F32, name=f"neg_ye{t}") for t in range(PACK)]
        y_unit = [keep.tile([P, S + PAD], F32, name=f"y_unit{t}") for t in range(PACK)]
        for window in neg_ye + y_unit:
            nc.gpsimd.memset(window[:, S:], 0.0)

        def round_weight(raw, t, grouped, copy):
            copy(
                grouped.rearrange("p (g c n slot) -> p g c slot n", slot=PACK, n=PAIR, c=GROUP // PAIR),
                raw[:].rearrange("p slot (g t c n) -> p t g c slot n", t=PACK, n=PAIR, c=GROUP // PAIR)[:, t],
            )

        def quantise(grouped, name, codes_buffer):
            width = grouped.shape[1] // PACK
            codes = keep.tile([P, width], U32, name=codes_buffer, align_bytes=MX_ALIGN)
            scales = keep.tile([P, width], U8, name=f"{name}_scales", align_bytes=MX_ALIGN)
            nc.vector.quantize_mx(out=codes[:].bitcast(FP8X4), scales=scales[:], in_=grouped)
            return codes, scales

        def pick_words(words, entries, name):
            picked = keep.tile([P, S], U32, name=name, align_bytes=MX_ALIGN)
            nc.vector.tensor_copy(picked[:], words[:].bitcast(U32).indirect(entries[:]))
            return picked

        def pick_scales(plane, entries, name):
            picked = keep.tile([P, S], U8, name=name, align_bytes=MX_ALIGN)
            nc.vector.tensor_copy(picked[:], plane[:].indirect(entries[:]))
            return picked

        def product(stationary, moving, bank, width):
            acc = psum.tile([P, width], F32, name=f"bank{bank}")
            nc.tensor.matmul_mx(
                out=acc[:],
                lhsT=stationary[0][:].bitcast(FP8X4),
                lhsT_scale=stationary[1][:],
                rhs=moving[0][:].bitcast(FP8X4),
                rhs_scale=moving[1][:],
                start=True,
                stop=True,
            )
            return acc

        def entries_of(list_sb, first, count):
            return list_sb[:, first // LIST_ROWS : (first + count) // LIST_ROWS]

        def interleaved(rows_by_tile):
            return rows_by_tile.rearrange("p t (c n) -> p c t n", n=PAIR)

        def as_words(grouped):
            return grouped.rearrange("p (c n t) -> p c t n", n=PAIR, t=PACK)

        e_picked = (pick_words(e_words_sb, ski_sb, "e_picked_words"), pick_scales(e_scales_sb, ski_sb, "e_picked_scales"))
        ye_acc = {}
        w2_bf = []
        for t in range(PACK):
            w2_bf.append(keep.tile([P, P * PACK], BF16, name=f"w2_bf{t}", align_bytes=MX_ALIGN))
            round_weight(w2_raw, t, w2_bf[t][:], nc.vector.tensor_copy if t % 2 == 0 else nc.scalar.copy)

        def skill_product(t, codes_buffer):
            ye_acc[t] = product(quantise(w2_bf[t][:], f"w2_{t}", codes_buffer), e_picked, t, S)

        for t in range(EARLY):
            skill_product(t, f"w2_codes{t}")

        skill = [keep.tile([P, PACK, HALF], F32, name=f"skill{half}") for half in range(2)]
        rest = {}

        def skill_rest(t, half):
            if half == 0:
                nc.scalar.activation(neg_ye[t][:, :S], ye_acc[t][:], COPY, scale=-1.0)
            rest[t, half] = keep.tile([P, HALF], F32, name=f"rest{t}_{half}", align_bytes=MX_ALIGN)
            neg_e2 = neg_ye[t][:].indirect(entries_of(sk2_sb, half * HALF, HALF))
            nc.vector.tensor_tensor(rest[t, half][:], neg_e2, att_sb[t][:, half * HALF : (half + 1) * HALF], ALU.add)

        def skill_term(t, half, buffer):
            neg_e1 = keep.tile([P, HALF], F32, name=buffer, align_bytes=MX_ALIGN)
            nc.scalar.activation(neg_e1[:], neg_ye[t][:].indirect(entries_of(sk1_sb, half * HALF, HALF)), COPY)
            nc.vector.scalar_tensor_tensor(
                skill[half][:, t, :], neg_e1[:], unit_sb[t][:], rest[t, half][:], ALU.mult, ALU.mult
            )

        def skill_tile(t):
            for half in range(2):
                skill_rest(t, half)
            for half in range(2):
                skill_term(t, half, f"neg_e1_{t}_{half}")

        for t in range(EARLY):
            skill_tile(t)

        last = EARLY - 1
        for t in range(EARLY, PACK):
            skill_product(t, f"neg_e1_{last}_{t - EARLY}")

        x_scales_picked = pick_scales(x_scales_sb, offs_sb, "x_picked_scales")
        x_picked = (pick_words(x_words_sb, offs_sb, "x_picked_words"), x_scales_picked)
        w1_bf = keep.tile([P, H * PACK], BF16, name="w1_bf", align_bytes=MX_ALIGN)
        for t in range(PACK):
            round_weight(w1_raw, t, w1_bf[:, t * P * PACK : (t + 1) * P * PACK], nc.scalar.copy)
        w1_codes, w1_scales = quantise(w1_bf[:], "w1", f"rest{last}_0")
        y_acc = []
        for t in range(PACK):
            tile_cols = slice(t * P, (t + 1) * P)
            y_acc.append(product((w1_codes[:, tile_cols], w1_scales[:, tile_cols]), x_picked, PACK + t, S))

        for t in range(EARLY, PACK):
            skill_rest(t, 0)
        for t in range(EARLY, PACK):
            skill_term(t, 0, f"neg_e1_{t}_0")
        for t in range(PACK):
            nc.scalar.activation(y_unit[t][:, :S], y_acc[t][:], COPY, scale=unit_sb[t][:])
        for t in range(EARLY, PACK):
            skill_rest(t, 1)

        w3_codes = keep.tile([P, N], U32, name="w3_codes", align_bytes=MX_ALIGN)
        w3_scales = keep.tile([P, N], U8, name="w3_scales", align_bytes=MX_ALIGN)
        exercise = [keep.tile([P, PACK, count], F32, name=f"exercise{c}") for c, (first, count) in enumerate(CHUNKS)]
        hid = [
            keep.tile([P, count * PACK], BF16, name=f"hid{c}", align_bytes=MX_ALIGN)
            for c, (first, count) in enumerate(CHUNKS)
        ]

        def exercise_term(c, t):
            first, count = CHUNKS[c]
            y_1 = y_unit[t][:].indirect(entries_of(ex_sb, first, count))
            if (c, t) != (0, 0):
                gathered = keep.tile([P, count], F32, name=f"y_1_{c}_{t}", align_bytes=MX_ALIGN)
                nc.scalar.activation(gathered[:], y_1, COPY)
                y_1 = gathered[:]
            nc.vector.tensor_tensor(exercise[c][:, t, :], y_1, att_sb[t][:, first : first + count], ALU.mult)

        def quantise_w3(buffer):
            w3_bf = keep.tile([P, N * PACK], BF16, name=buffer, align_bytes=MX_ALIGN)
            nc.scalar.copy(as_words(w3_bf[:]), interleaved(w3_raw[:]))
            nc.vector.quantize_mx(out=w3_codes[:].bitcast(FP8X4), scales=w3_scales[:], in_=w3_bf[:])

        def combine(c):
            first, count = CHUNKS[c]
            skill_cols = skill[first // HALF][:, :, first % HALF : first % HALF + count]
            nc.vector.tensor_tensor(
                as_words(hid[c][:]), interleaved(exercise[c][:]), interleaved(skill_cols), ALU.subtract
            )

        def finish(c):
            first, count = CHUNKS[c]
            hid_mx = quantise(hid[c][:], f"hid{c}", f"hid{c}_codes")
            for m in range(N // P):
                rows = slice(m * P, (m + 1) * P)
                acc = product((w3_codes[:, rows], w3_scales[:, rows]), hid_mx, (N // P) * c + m, count)
                result = keep.tile([P, count], F32, name=f"result{c}_{m}")
                if c == len(CHUNKS) - 1 and m == N // P - 1:
                    nc.vector.tensor_copy(result[:], acc[:])
                else:
                    nc.scalar.copy(result[:], acc[:])
                nc.sync.dma_start(out[rows, first : first + count], result[:])

        for t in range(PACK):
            exercise_term(0, t)
        skill_term(EARLY, 1, "y_1_0_1")
        combine(0)
        skill_term(EARLY + 1, 1, "y_1_0_2")
        quantise_w3("y_1_0_3")
        finish(0)
        exercise_term(1, 0)
        exercise_term(1, 1)
        for c in range(1, len(CHUNKS)):
            more = c + 1 < len(CHUNKS)
            exercise_term(c, 2)
            exercise_term(c, 3)
            if more:
                exercise_term(c + 1, 0)
            combine(c)
            if more:
                exercise_term(c + 1, 1)
            finish(c)
